import numpy as np
import ml_dtypes


def mxq(x, axis, fmt="e4m3"):
    dtype, down = {"e4m3": (ml_dtypes.float8_e4m3fn, 7), "e5m2": (ml_dtypes.float8_e5m2, 14)}[fmt]
    v = np.moveaxis(np.asarray(x, np.float32).astype(ml_dtypes.bfloat16).astype(np.float64), axis, -1)
    blocks = v.reshape(v.shape[:-1] + (-1, 32))
    amax = np.abs(blocks).max(-1, keepdims=True)
    byte = np.maximum(np.where(amax > 0, np.frexp(amax)[1] - 1 + 127, 0) - down, 1)
    scale = np.exp2(byte - 127.0)
    codes = (blocks / scale).astype(np.float32).astype(dtype).astype(np.float64)
    return np.moveaxis((codes * scale).reshape(v.shape), -1, axis)


WIDE = False


def mx_kscale(k):
    if not WIDE:
        return np.ones(k)
    levels = np.array([10, -10, 5, -5, 0])
    if k % 512:
        return np.exp2(np.random.permutation(np.resize(levels, k // 32))).repeat(32)
    a = np.empty((k // 512, 16))
    for p in range(k // 512):
        a[p, :8] = np.random.permutation(np.resize(levels, 8))
        for g in range(8):
            far = levels[np.abs(levels - a[p, g]) >= 10]
            a[p, g + 8] = far[np.random.randint(len(far))]
    return np.exp2(a.ravel()).repeat(32)


def f64(x):
    return np.asarray(x).astype(np.float64)


def striped(idx):
    return np.tile(idx.reshape(-1, 16).T, (8, 1)).astype(np.uint16)


def unstriped(offs):
    return offs[:16].T.reshape(-1).astype(np.int64)


def striped8(idx):
    return np.concatenate([x.reshape(-1, 16).T for x in idx]).astype(np.uint16)


def runs(offs, k):
    lists = np.stack([offs[16 * r : 16 * r + 16].T.reshape(-1) for r in range(8)]).astype(np.int64)
    return lists[np.arange(k) % 512 // 64]


def pack_weight(w):
    k, n = w.shape
    w = f64(np.asarray(w, np.float32).astype(ml_dtypes.bfloat16)).reshape(k // 32, 32, n)
    amax = np.abs(w).max(1)
    byte = np.clip(np.where(amax > 0, np.frexp(amax)[1] - 1 + 127 - 7, 1), 1, 254)
    scaled = (w * np.exp2(127.0 - byte)[:, None, :]).reshape(k, n).astype(np.float32)
    words = np.ascontiguousarray(scaled.reshape(k // 512, 128, 4, n).transpose(0, 1, 3, 2)).astype(ml_dtypes.float8_e4m3fn).view(np.uint8)
    return words, np.ascontiguousarray(byte.astype(np.uint8).reshape(k // 512, 16, n))


def unpack_weight(words, scales):
    g, p, n, _ = words.shape
    vals = np.ascontiguousarray(words).view(ml_dtypes.float8_e4m3fn).astype(np.float64) * np.repeat(np.exp2(scales.astype(np.float64) - 127.0), 8, axis=1)[..., None]
    return vals.transpose(0, 1, 3, 2).reshape(g * 512, n)

def planes(y):
    n, m = y.shape
    v = y.astype(np.float32).astype(ml_dtypes.bfloat16).astype(np.float64).reshape(n // 32, 32, m)
    top = np.abs(v).max(1)
    byte = np.clip(np.where(top > 0, np.frexp(top)[1] - 1 + 127 - 7, 1), 1, 254)
    codes = (v * np.exp2(127.0 - byte)[:, None, :]).reshape(n, m).astype(np.float32).astype(ml_dtypes.float8_e4m3fn).view(np.uint8)
    words = codes.reshape(n // 512, 128, 4, m).transpose(0, 1, 3, 2)
    return np.ascontiguousarray(words), np.ascontiguousarray(byte.astype(np.uint8).reshape(n // 512, 16, m))


K, T, S, N, G, H, W, U = 512, 2048, 512, 512, 2048, 512, 1024, 384


def setup_inputs():
    n = np.random.standard_normal
    s = mx_kscale(K)[:, None]
    u = mx_kscale(S)
    packed_xT = pack_weight(n((K, T)) * s)
    packed_dT = pack_weight(n((K, G)) / s)
    packed_w1 = pack_weight(n((H, N)) / np.sqrt(2 * H) / u[:, None])
    packed_w2 = pack_weight(n((K, N)) / np.sqrt(2 * K) / s)
    return {
        "x_words": packed_xT[0],
        "x_scales": packed_xT[1],
        "d_words": packed_dT[0],
        "d_scales": packed_dT[1],
        "gn": (np.random.uniform(0.5, 1.5, (H, 1)) * u[:, None]).astype(np.float32),
        "w1_words": packed_w1[0],
        "w1_scales": packed_w1[1],
        "w2_words": packed_w2[0],
        "w2_scales": packed_w2[1],
        "offs": striped(np.random.permutation(T)[:S]),
        "k1": striped8(np.random.randint(0, G, (8, H))),
        "n1": striped(np.random.randint(0, S, W)),
        "two": striped(np.random.permutation(T)[:S]),
        "n2": striped(np.random.permutation(S)[:U]),
        "n3": striped(np.random.permutation(S)[:U]),
    }


def reference(x_words, x_scales, d_words, d_scales, gn, w1_words, w1_scales, w2_words, w2_scales, offs, k1, n1, two, n2, n3):
    d_k1 = unpack_weight(d_words, d_scales)[np.arange(K)[:, None], runs(k1, K)]
    xq = unpack_weight(x_words, x_scales)[:, unstriped(offs)]
    s = 0.0625 * (d_k1.T @ xq)
    mb = s[:, unstriped(n1)]
    ms = mb.reshape(H, S, 2).sum(axis=2)
    mx = mb.reshape(H, S, 2).max(axis=2)
    z = f64(gn) * (ms - np.maximum(s, mx))
    x_two = unpack_weight(x_words, x_scales)[:, unstriped(two)]
    h = unpack_weight(w1_words, w1_scales).T @ mxq(z, 0, "e4m3") + unpack_weight(w2_words, w2_scales).T @ x_two
    old = h[:, unstriped(n2)]
    pa = h[:, unstriped(n3)]
    ra = old - (0.5 * pa)
    out = h.copy()
    out[:, unstriped(n2)] = ra
    return (out,) + planes(out)

@@ -1,0 +1,268 @@
+from contextlib import ExitStack
+
+import concourse.mybir as mybir
+
+K, T, S, N, G, H, W, U = 512, 2048, 512, 512, 2048, 512, 1024, 384
+FLOPS = 3 * 2 * 512 * 512 * 512
+
+F32 = mybir.dt.float32
+BF16 = mybir.dt.bfloat16
+I32 = mybir.dt.int32
+U32 = mybir.dt.uint32
+U16 = mybir.dt.uint16
+U8 = mybir.dt.uint8
+FP8X4 = mybir.dt.float8_e4m3fn_x4
+ALU = mybir.AluOpType
+COPY = mybir.ActivationFunctionType.Copy
+
+P = 128
+PACK = 4
+CH = 256
+NCH = S // CH
+S_WIN = 544
+H_WIN = 768
+
+
+def tile_picked_kmixgpairkdif_none_po_kernel(
+    tc, x_words, x_scales, d_words, d_scales, gn, w1_words, w1_scales, w2_words, w2_scales,
+    offs, k1, n1, two, n2, n3, out_0, out_1, out_2,
+):
+    nc = tc.nc
+    with ExitStack() as ctx:
+        keep = ctx.enter_context(tc.tile_pool(name="keep", bufs=1))
+        psum = ctx.enter_context(tc.psum_pool(name="psum", bufs=1))
+
+        def sb(shape, dtype, name):
+            return keep.tile(shape, dtype, name=name, align_bytes=64)
+
+        def words_view(dram):
+            return dram[0].rearrange("p n t -> p (n t)").bitcast(I32)
+
+        def load_list(dram, n, name):
+            t = keep.tile([P, n // 16], U16, name=name)
+            nc.sync.dma_start(t[:], dram)
+            return t
+
+        d_sc = sb([P, G], U8, "d_sc")
+        x_sc = sb([P, T], U8, "x_sc")
+        nc.vector.memset(d_sc[:].bitcast(I32), 0)
+        nc.vector.memset(x_sc[:].bitcast(I32), 0)
+        gain = sb([P, PACK], F32, "gain")
+        nc.gpsimd.dma_start(gain[:], gn.rearrange("(p t) o -> p (t o)", t=PACK))
+
+        k1_sb = load_list(k1, H, "k1_sb")
+        offs_sb = load_list(offs, S, "offs_sb")
+        two_sb = load_list(two, S, "two_sb")
+        n1_sb = load_list(n1, W, "n1_sb")
+        n2_sb = load_list(n2, U, "n2_sb")
+        n3_sb = load_list(n3, U, "n3_sb")
+        nc.sync.dma_start(d_sc[:].bitcast(I32)[0:P:8, :], d_scales[0].bitcast(I32))
+        d_w = sb([P, G], U32, "d_w")
+        nc.sync.dma_start(d_w[:].bitcast(I32), words_view(d_words))
+        for r in range(4):
+            nc.sync.dma_start(x_sc[:].bitcast(I32)[r:P:32, :], x_scales[0].bitcast(I32)[r:16:4, :])
+        x_w = sb([P, T], U32, "x_w")
+        nc.sync.dma_start(x_w[:].bitcast(I32), words_view(x_words))
+
+        s_win = [sb([P, S_WIN], F32, f"s_win{t}") for t in range(PACK)]
+        h_win = [sb([P, H_WIN], F32, f"h_win{t}") for t in range(PACK)]
+        for t in range(PACK):
+            nc.gpsimd.memset(s_win[t][:, S:S_WIN], 0.0)
+            nc.gpsimd.memset(h_win[t][:, S:H_WIN], 0.0)
+
+        gain16 = sb([P, PACK], F32, "gain16")
+        nc.scalar.activation(gain16[:], gain[:], COPY, scale=0.0625)
+
+        def deal(dst, src):
+            nc.vector.tensor_copy(
+                dst.rearrange("p (w t m) -> p w m t", t=PACK, m=P),
+                src.rearrange("p (w m t) -> p w m t", t=PACK, m=P),
+            )
+
+        dk_sc_raw = sb([P, H], U8, "dk_sc_raw")
+        nc.vector.tensor_copy(dk_sc_raw[:], d_sc[:].indirect(k1_sb[:]))
+        dk_sc_dealt = sb([P, H], U8, "dk_sc_dealt")
+        deal(dk_sc_dealt[:], dk_sc_raw[:])
+        dk_sc = sb([P, H], U8, "dk_sc")
+        nc.vector.tensor_copy(dk_sc[:].bitcast(I32), dk_sc_dealt[:].bitcast(I32))
+        for r in range(1, 4):
+            nc.scalar.dma_start(dk_sc[:].bitcast(I32)[r:P:32, :], dk_sc_dealt[:].bitcast(I32)[8 * r : P : 32, :])
+        w_sc = sb([P, N], U8, "dk_sc_dealt")
+        nc.gpsimd.memset(w_sc[:].bitcast(I32), 0)
+        for j, sc in enumerate((w1_scales, w2_scales)):
+            for q in range(4):
+                nc.sync.dma_start(
+                    w_sc[:].bitcast(I32)[32 * q + 4 * j : 32 * q + 4 * j + 4, :],
+                    sc[0].bitcast(I32)[4 * q : 4 * q + 4, :],
+                )
+
+        dk_w_raw = sb([P, H], U32, "dk_w_raw")
+        nc.vector.tensor_copy(dk_w_raw[:], d_w[:].indirect(k1_sb[:]))
+        w_w = sb([P, 2 * N], U32, "d_w")
+        nc.sync.dma_start(w_w[:, 0:N].bitcast(I32), words_view(w1_words))
+        nc.sync.dma_start(w_w[:, N : 2 * N].bitcast(I32), words_view(w2_words))
+        dk_w = sb([P, H], U32, "dk_w")
+        deal(dk_w[:].bitcast(I32), dk_w_raw[:].bitcast(I32))
+        xq_sc = sb([P, S], U8, "xq_sc")
+        nc.vector.tensor_copy(xq_sc[:], x_sc[:].indirect(offs_sb[:]))
+        xq_w = sb([P, S], U32, "xq_w")
+        nc.vector.tensor_copy(xq_w[:], x_w[:].indirect(offs_sb[:]))
+
+        s_ps = []
+        for t in range(PACK):
+            ps = psum.tile([P, S], F32, name=f"bank{t}")
+            cols = slice(P * t, P * (t + 1))
+            nc.tensor.matmul_mx(ps[:], lhsT=dk_w[:, cols].bitcast(FP8X4), lhsT_scale=dk_sc[:, cols],
+                                rhs=xq_w[:].bitcast(FP8X4), rhs_scale=xq_sc[:], start=True, stop=True)
+            s_ps.append(ps)
+
+        x2_w = sb([P, S], U32, "x2_w")
+        nc.vector.tensor_copy(x2_w[:], x_w[:].indirect(two_sb[:]))
+        wd_w = sb([P, 2 * N], U32, "wd_w")
+        wd_sc = sb([P, N], U8, "wd_sc")
+        nc.scalar.activation(s_win[0][:, 0:S], s_ps[0][:], COPY)
+        for t in range(1, PACK):
+            nc.vector.tensor_copy(s_win[t][:, 0:S], s_ps[t][:])
+        x2_sc = sb([P, S], U8, "x2_sc")
+        nc.vector.tensor_copy(x2_sc[:], x_sc[:].indirect(two_sb[:]))
+        deal(wd_w[:].bitcast(I32), w_w[:].bitcast(I32))
+
+        units = [(c, t) for c in range(NCH) for t in range(PACK)]
+        members = [sb([P, 2 * CH], F32, f"members{u}") for u in range(len(units))]
+        top = [sb([P, CH], F32, f"top{u}") for u in range(len(units))]
+        gap = [sb([P, CH], F32, f"gap{u}") for u in range(len(units))]
+        diff = [sb([P, CH], F32, f"diff{u}") for u in range(len(units))]
+        z_rows = sb([P, PACK * CH], BF16, "z_rows")
+        z_grp = [sb([P, PACK * CH], BF16, f"z_grp{c}") for c in range(NCH)]
+        z_w = [sb([P, CH], U32, f"z_w{c}") for c in range(NCH)]
+        z_sc = [sb([P, CH], U8, f"z_sc{c}") for c in range(NCH)]
+        h_ps = {}
+
+        def interleave(eng_copy, dst, src):
+            eng_copy(dst.rearrange("p (c i t) -> p c t i", i=4, t=PACK), src.rearrange("p t (c i) -> p c t i", i=4))
+
+        def fetch(u):
+            c, t = units[u]
+            nc.scalar.activation(members[u][:], s_win[t][:].indirect(n1_sb[:, c * CH // 8 : (c + 1) * CH // 8]), COPY)
+
+        def op_top(u):
+            c, t = units[u]
+            nc.vector.tensor_tensor(top[u][:], members[u][:, 1::2], s_win[t][:, c * CH : (c + 1) * CH], ALU.max)
+
+        def op_gap(u):
+            nc.vector.tensor_tensor(gap[u][:], members[u][:, 0::2], top[u][:], ALU.subtract)
+
+        def op_diff(u):
+            nc.vector.scalar_tensor_tensor(diff[u][:], gap[u][:], 0.0, members[u][:, 1::2], ALU.min, ALU.add)
+
+        def gain_rows(t):
+            nc.scalar.activation(z_rows[:, t * CH : (t + 1) * CH], diff[t][:], COPY, scale=gain16[:, t : t + 1])
+
+        def gain_grouped(t):
+            nc.vector.tensor_scalar(z_grp[1][:, t::PACK], diff[PACK + t][:], gain16[:, t : t + 1], None, ALU.mult)
+
+        def quant_z(c):
+            nc.vector.quantize_mx(z_w[c][:].bitcast(FP8X4), z_sc[c][:], z_grp[c][:])
+
+        def open_h(c, t):
+            ccols = slice(c * CH, (c + 1) * CH)
+            ps = psum.tile([P, CH], F32, name=f"bank{(4 * (1 - c)) + t}")
+            h_ps[c, t] = ps
+            nc.tensor.matmul_mx(ps[:], lhsT=wd_w[:, N + P * t : N + P * (t + 1)].bitcast(FP8X4),
+                                lhsT_scale=wd_sc[4:P, P * t : P * (t + 1)],
+                                rhs=x2_w[:, ccols].bitcast(FP8X4), rhs_scale=x2_sc[:, ccols], start=True, stop=False)
+
+        def close_h(c, t):
+            nc.tensor.matmul_mx(h_ps[c, t][:], lhsT=wd_w[:, P * t : P * (t + 1)].bitcast(FP8X4),
+                                lhsT_scale=wd_sc[:, P * t : P * (t + 1)],
+                                rhs=z_w[c][:].bitcast(FP8X4), rhs_scale=z_sc[c][:], start=False, stop=True)
+
+        for u in range(len(units)):
+            fetch(u)
+        for u in range(len(units) + 1):
+            if u < len(units):
+                op_top(u)
+            if u > 0:
+                op_diff(u - 1)
+            if u < len(units):
+                op_gap(u)
+            if u == 1:
+                deal(wd_sc[:], w_sc[:])
+                for c in range(NCH):
+                    for t in range(PACK):
+                        open_h(c, t)
+            if u == PACK:
+                for t in range(PACK):
+                    gain_rows(t)
+                interleave(nc.scalar.copy, z_grp[0][:], z_rows[:].rearrange("p (t c) -> p t c", t=PACK))
+            if u == len(units):
+                quant_z(0)
+            if u > PACK:
+                gain_grouped(u - 1 - PACK)
+        quant_z(1)
+        for t in range(PACK):
+            close_h(0, t)
+            close_h(1, t)
+
+        old = [sb([P, U], F32, f"old{t}") for t in range(PACK)]
+        pull = [sb([P, U], F32, f"pull{t}") for t in range(PACK)]
+        o_rows = sb([P, PACK * S], BF16, "o_rows")
+        out_rows = out_0.rearrange("(p t) c -> p t c", t=PACK)
+
+        def pull_of(t):
+            nc.scalar.activation(pull[t][:], h_win[t][:].indirect(n3_sb[:]), COPY, scale=-0.5)
+
+        def old_of(t):
+            nc.scalar.activation(old[t][:], h_win[t][:].indirect(n2_sb[:]), COPY)
+
+        def put(t):
+            nc.vector.tensor_tensor(h_win[t][:].indirect(n2_sb[:]), old[t][:], pull[t][:], ALU.add)
+
+        def store(t):
+            nc.sync.dma_start(out_rows[:, t, :], h_win[t][:, 0:S])
+
+        def h_out(eng_copy, t):
+            for c in range(NCH):
+                eng_copy(h_win[t][:, c * CH : (c + 1) * CH], h_ps[c, t][:])
+
+        def round_rows(eng_copy, t):
+            eng_copy(o_rows[:, t * S : (t + 1) * S], h_win[t][:, 0:S])
+
+        h_out(nc.scalar.copy, 0)
+        h_out(nc.vector.tensor_copy, 1)
+        pull_of(0)
+        nc.vector.tensor_copy(old[0][:], h_win[0][:].indirect(n2_sb[:]))
+        put(0)
+        store(0)
+        h_out(nc.scalar.copy, 3)
+        pull_of(3)
+        nc.vector.tensor_tensor(old[3][:], h_win[3][:].indirect(n2_sb[:]), pull[3][:], ALU.add)
+        old_of(1)
+        pull_of(1)
+        put(1)
+        store(1)
+        h_out(nc.scalar.copy, 2)
+        old_of(2)
+        pull_of(2)
+        put(2)
+        store(2)
+        nc.scalar.activation(h_win[3][:].indirect(n2_sb[:]), old[3][:], COPY)
+        store(3)
+        round_rows(nc.scalar.copy, 0)
+        round_rows(nc.scalar.copy, 3)
+        round_rows(nc.vector.tensor_copy, 1)
+        round_rows(nc.vector.tensor_copy, 2)
+
+        o_grp = [sb([P, PACK * CH], BF16, f"o_grp{c}") for c in range(2)]
+        o_w = sb([P, S], U32, "o_w")
+        o_sc = sb([P, S], U8, "o_sc")
+        o_view = o_rows[:].rearrange("p (t c) -> p t c", t=PACK)
+        interleave(nc.vector.tensor_copy, o_grp[0][:], o_view[:, :, 0:CH])
+        interleave(nc.scalar.copy, o_grp[1][:], o_view[:, :, CH:S])
+        for c in range(2):
+            ccols = slice(c * CH, (c + 1) * CH)
+            nc.vector.quantize_mx(o_w[:, ccols].bitcast(FP8X4), o_sc[:, ccols], o_grp[c][:])
+            nc.sync.dma_start(words_view(out_1)[:, ccols], o_w[:, ccols].bitcast(I32))
+        for q in range(4):
+            eng = nc.sync if q % 2 == 0 else nc.scalar
+            eng.dma_start(out_2[0].bitcast(I32)[4 * q : 4 * q + 4, :], o_sc[:].bitcast(I32)[32 * q : 32 * q + 4, :])

@@ -21,6 +21,7 @@ CH = 256
 NCH = S // CH
 S_WIN = 544
 H_WIN = 768
+SPLIT = 320
 
 
 def tile_picked_kmixgpairkdif_none_po_kernel(
@@ -45,24 +46,24 @@ def tile_picked_kmixgpairkdif_none_po_kernel(
 
         d_sc = sb([P, G], U8, "d_sc")
         x_sc = sb([P, T], U8, "x_sc")
-        nc.vector.memset(d_sc[:].bitcast(I32), 0)
+        nc.gpsimd.memset(d_sc[:].bitcast(I32), 0)
         nc.vector.memset(x_sc[:].bitcast(I32), 0)
-        gain = sb([P, PACK], F32, "gain")
-        nc.gpsimd.dma_start(gain[:], gn.rearrange("(p t) o -> p (t o)", t=PACK))
 
         k1_sb = load_list(k1, H, "k1_sb")
+        nc.sync.dma_start(d_sc[:].bitcast(I32)[0:P:8, :], d_scales[0].bitcast(I32))
+        for r in range(4):
+            nc.sync.dma_start(x_sc[:].bitcast(I32)[r:P:32, :], x_scales[0].bitcast(I32)[r:16:4, :])
         offs_sb = load_list(offs, S, "offs_sb")
+        d_w = sb([P, G], U32, "d_w")
+        nc.sync.dma_start(d_w[:].bitcast(I32), words_view(d_words))
+        x_w = sb([P, T], U32, "x_w")
+        nc.sync.dma_start(x_w[:].bitcast(I32), words_view(x_words))
         two_sb = load_list(two, S, "two_sb")
         n1_sb = load_list(n1, W, "n1_sb")
         n2_sb = load_list(n2, U, "n2_sb")
         n3_sb = load_list(n3, U, "n3_sb")
-        nc.sync.dma_start(d_sc[:].bitcast(I32)[0:P:8, :], d_scales[0].bitcast(I32))
-        d_w = sb([P, G], U32, "d_w")
-        nc.sync.dma_start(d_w[:].bitcast(I32), words_view(d_words))
-        for r in range(4):
-            nc.sync.dma_start(x_sc[:].bitcast(I32)[r:P:32, :], x_scales[0].bitcast(I32)[r:16:4, :])
-        x_w = sb([P, T], U32, "x_w")
-        nc.sync.dma_start(x_w[:].bitcast(I32), words_view(x_words))
+        gain = sb([P, PACK], F32, "gain")
+        nc.gpsimd.dma_start(gain[:], gn.rearrange("(p t) o -> p (t o)", t=PACK))
 
         s_win = [sb([P, S_WIN], F32, f"s_win{t}") for t in range(PACK)]
         h_win = [sb([P, H_WIN], F32, f"h_win{t}") for t in range(PACK)]
@@ -87,15 +88,9 @@ def tile_picked_kmixgpairkdif_none_po_kernel(
         nc.vector.tensor_copy(dk_sc[:].bitcast(I32), dk_sc_dealt[:].bitcast(I32))
         for r in range(1, 4):
             nc.scalar.dma_start(dk_sc[:].bitcast(I32)[r:P:32, :], dk_sc_dealt[:].bitcast(I32)[8 * r : P : 32, :])
-        w_sc = sb([P, N], U8, "dk_sc_dealt")
-        nc.gpsimd.memset(w_sc[:].bitcast(I32), 0)
-        for j, sc in enumerate((w1_scales, w2_scales)):
-            for q in range(4):
-                nc.sync.dma_start(
-                    w_sc[:].bitcast(I32)[32 * q + 4 * j : 32 * q + 4 * j + 4, :],
-                    sc[0].bitcast(I32)[4 * q : 4 * q + 4, :],
-                )
 
+        xq_sc = sb([P, S], U8, "xq_sc")
+        nc.vector.tensor_copy(xq_sc[:], x_sc[:].indirect(offs_sb[:]))
         dk_w_raw = sb([P, H], U32, "dk_w_raw")
         nc.vector.tensor_copy(dk_w_raw[:], d_w[:].indirect(k1_sb[:]))
         w_w = sb([P, 2 * N], U32, "d_w")
@@ -103,8 +98,14 @@ def tile_picked_kmixgpairkdif_none_po_kernel(
         nc.sync.dma_start(w_w[:, N : 2 * N].bitcast(I32), words_view(w2_words))
         dk_w = sb([P, H], U32, "dk_w")
         deal(dk_w[:].bitcast(I32), dk_w_raw[:].bitcast(I32))
-        xq_sc = sb([P, S], U8, "xq_sc")
-        nc.vector.tensor_copy(xq_sc[:], x_sc[:].indirect(offs_sb[:]))
+        w_sc = sb([P, N], U8, "dk_w_raw")
+        nc.gpsimd.memset(w_sc[:].bitcast(I32), 0)
+        for j, sc in enumerate((w1_scales, w2_scales)):
+            for q in range(4):
+                nc.sync.dma_start(
+                    w_sc[:].bitcast(I32)[32 * q + 4 * j : 32 * q + 4 * j + 4, :],
+                    sc[0].bitcast(I32)[4 * q : 4 * q + 4, :],
+                )
         xq_w = sb([P, S], U32, "xq_w")
         nc.vector.tensor_copy(xq_w[:], x_w[:].indirect(offs_sb[:]))
 
@@ -120,12 +121,12 @@ def tile_picked_kmixgpairkdif_none_po_kernel(
         nc.vector.tensor_copy(x2_w[:], x_w[:].indirect(two_sb[:]))
         wd_w = sb([P, 2 * N], U32, "wd_w")
         wd_sc = sb([P, N], U8, "wd_sc")
+        deal(wd_w[:].bitcast(I32), w_w[:].bitcast(I32))
         nc.scalar.activation(s_win[0][:, 0:S], s_ps[0][:], COPY)
-        for t in range(1, PACK):
+        for t in (1, 2):
             nc.vector.tensor_copy(s_win[t][:, 0:S], s_ps[t][:])
         x2_sc = sb([P, S], U8, "x2_sc")
         nc.vector.tensor_copy(x2_sc[:], x_sc[:].indirect(two_sb[:]))
-        deal(wd_w[:].bitcast(I32), w_w[:].bitcast(I32))
 
         units = [(c, t) for c in range(NCH) for t in range(PACK)]
         members = [sb([P, 2 * CH], F32, f"members{u}") for u in range(len(units))]
@@ -140,6 +141,12 @@ def tile_picked_kmixgpairkdif_none_po_kernel(
 
         def interleave(eng_copy, dst, src):
             eng_copy(dst.rearrange("p (c i t) -> p c t i", i=4, t=PACK), src.rearrange("p t (c i) -> p c t i", i=4))
+
+        def interleave_scalar(dst, src):
+            nc.scalar.copy(dst.rearrange("p (c t) -> p c t", t=PACK), src.rearrange("p t c -> p c t"))
+
+        def interleave_vector(dst, src):
+            interleave(nc.vector.tensor_copy, dst, src)
 
         def fetch(u):
             c, t = units[u]
@@ -156,10 +163,13 @@ def tile_picked_kmixgpairkdif_none_po_kernel(
             nc.vector.scalar_tensor_tensor(diff[u][:], gap[u][:], 0.0, members[u][:, 1::2], ALU.min, ALU.add)
 
         def gain_rows(t):
-            nc.scalar.activation(z_rows[:, t * CH : (t + 1) * CH], diff[t][:], COPY, scale=gain16[:, t : t + 1])
+            nc.vector.tensor_scalar(z_rows[:, t * CH : (t + 1) * CH], diff[t][:], gain16[:, t : t + 1], None, ALU.mult)
 
         def gain_grouped(t):
-            nc.vector.tensor_scalar(z_grp[1][:, t::PACK], diff[PACK + t][:], gain16[:, t : t + 1], None, ALU.mult)
+            if t < 2:
+                nc.scalar.activation(z_grp[1][:, t::PACK], diff[PACK + t][:], COPY, scale=gain16[:, t : t + 1])
+            else:
+                nc.vector.tensor_scalar(z_grp[1][:, t::PACK], diff[PACK + t][:], gain16[:, t : t + 1], None, ALU.mult)
 
         def quant_z(c):
             nc.vector.quantize_mx(z_w[c][:].bitcast(FP8X4), z_sc[c][:], z_grp[c][:])
@@ -178,6 +188,8 @@ def tile_picked_kmixgpairkdif_none_po_kernel(
                                 rhs=z_w[c][:].bitcast(FP8X4), rhs_scale=z_sc[c][:], start=False, stop=True)
 
         for u in range(len(units)):
+            if u == 2:
+                nc.scalar.activation(s_win[3][:, 0:S], s_ps[3][:], COPY)
             fetch(u)
         for u in range(len(units) + 1):
             if u < len(units):
@@ -186,27 +198,28 @@ def tile_picked_kmixgpairkdif_none_po_kernel(
                 op_diff(u - 1)
             if u < len(units):
                 op_gap(u)
+            if 0 < u <= PACK:
+                gain_rows(u - 1)
             if u == 1:
                 deal(wd_sc[:], w_sc[:])
                 for c in range(NCH):
                     for t in range(PACK):
                         open_h(c, t)
             if u == PACK:
-                for t in range(PACK):
-                    gain_rows(t)
-                interleave(nc.scalar.copy, z_grp[0][:], z_rows[:].rearrange("p (t c) -> p t c", t=PACK))
-            if u == len(units):
-                quant_z(0)
+                interleave_scalar(z_grp[0][:], z_rows[:].rearrange("p (t c) -> p t c", t=PACK))
             if u > PACK:
                 gain_grouped(u - 1 - PACK)
+            if u == len(units) - 1:
+                quant_z(0)
+                for t in range(PACK):
+                    close_h(0, t)
+                    nc.scalar.copy(h_win[t][:, 0:CH], h_ps[0, t][:])
         quant_z(1)
-        for t in range(PACK):
-            close_h(0, t)
+        for t in (0, 1, 3, 2):
             close_h(1, t)
 
         old = [sb([P, U], F32, f"old{t}") for t in range(PACK)]
         pull = [sb([P, U], F32, f"pull{t}") for t in range(PACK)]
-        o_rows = sb([P, PACK * S], BF16, "o_rows")
         out_rows = out_0.rearrange("(p t) c -> p t c", t=PACK)
 
         def pull_of(t):
@@ -222,10 +235,9 @@ def tile_picked_kmixgpairkdif_none_po_kernel(
             nc.sync.dma_start(out_rows[:, t, :], h_win[t][:, 0:S])
 
         def h_out(eng_copy, t):
-            for c in range(NCH):
-                eng_copy(h_win[t][:, c * CH : (c + 1) * CH], h_ps[c, t][:])
+            eng_copy(h_win[t][:, CH:S], h_ps[1, t][:])
 
-        def round_rows(eng_copy, t):
+        def round_rows(eng_copy, o_rows, t):
             eng_copy(o_rows[:, t * S : (t + 1) * S], h_win[t][:, 0:S])
 
         h_out(nc.scalar.copy, 0)
@@ -235,33 +247,34 @@ def tile_picked_kmixgpairkdif_none_po_kernel(
         put(0)
         store(0)
         h_out(nc.scalar.copy, 3)
+        h_out(nc.scalar.copy, 2)
         pull_of(3)
         nc.vector.tensor_tensor(old[3][:], h_win[3][:].indirect(n2_sb[:]), pull[3][:], ALU.add)
         old_of(1)
         pull_of(1)
         put(1)
         store(1)
-        h_out(nc.scalar.copy, 2)
         old_of(2)
         pull_of(2)
         put(2)
         store(2)
         nc.scalar.activation(h_win[3][:].indirect(n2_sb[:]), old[3][:], COPY)
         store(3)
-        round_rows(nc.scalar.copy, 0)
-        round_rows(nc.scalar.copy, 3)
-        round_rows(nc.vector.tensor_copy, 1)
-        round_rows(nc.vector.tensor_copy, 2)
+        o_rows = sb([P, PACK * S], BF16, "old3")
+        round_rows(nc.scalar.copy, o_rows, 0)
+        round_rows(nc.scalar.copy, o_rows, 3)
+        round_rows(nc.vector.tensor_copy, o_rows, 1)
+        round_rows(nc.vector.tensor_copy, o_rows, 2)
 
-        o_grp = [sb([P, PACK * CH], BF16, f"o_grp{c}") for c in range(2)]
+        o_grp = sb([P, PACK * S], BF16, "o_grp")
         o_w = sb([P, S], U32, "o_w")
         o_sc = sb([P, S], U8, "o_sc")
         o_view = o_rows[:].rearrange("p (t c) -> p t c", t=PACK)
-        interleave(nc.vector.tensor_copy, o_grp[0][:], o_view[:, :, 0:CH])
-        interleave(nc.scalar.copy, o_grp[1][:], o_view[:, :, CH:S])
+        for regroup, lo, hi in ((interleave_vector, 0, CH), (interleave_scalar, SPLIT, S), (interleave_vector, CH, SPLIT)):
+            regroup(o_grp[:, PACK * lo : PACK * hi], o_view[:, :, lo:hi])
         for c in range(2):
             ccols = slice(c * CH, (c + 1) * CH)
-            nc.vector.quantize_mx(o_w[:, ccols].bitcast(FP8X4), o_sc[:, ccols], o_grp[c][:])
+            nc.vector.quantize_mx(o_w[:, ccols].bitcast(FP8X4), o_sc[:, ccols], o_grp[:, PACK * c * CH : PACK * (c + 1) * CH])
             nc.sync.dma_start(words_view(out_1)[:, ccols], o_w[:, ccols].bitcast(I32))
         for q in range(4):
             eng = nc.sync if q % 2 == 0 else nc.scalar

from contextlib import ExitStack

import concourse.mybir as mybir

K, T, S, N, G, H, W, U = 512, 2048, 512, 512, 2048, 512, 1024, 384
FLOPS = 3 * 2 * 512 * 512 * 512

F32 = mybir.dt.float32
BF16 = mybir.dt.bfloat16
I32 = mybir.dt.int32
U32 = mybir.dt.uint32
U16 = mybir.dt.uint16
U8 = mybir.dt.uint8
FP8X4 = mybir.dt.float8_e4m3fn_x4
ALU = mybir.AluOpType
COPY = mybir.ActivationFunctionType.Copy

P = 128
PACK = 4
CH = 256
NCH = S // CH
S_WIN = 544
H_WIN = 768
SPLIT = 320


def tile_picked_kmixgpairkdif_none_po_kernel(
    tc, x_words, x_scales, d_words, d_scales, gn, w1_words, w1_scales, w2_words, w2_scales,
    offs, k1, n1, two, n2, n3, out_0, out_1, out_2,
):
    nc = tc.nc
    with ExitStack() as ctx:
        keep = ctx.enter_context(tc.tile_pool(name="keep", bufs=1))
        psum = ctx.enter_context(tc.psum_pool(name="psum", bufs=1))

        def sb(shape, dtype, name):
            return keep.tile(shape, dtype, name=name, align_bytes=64)

        def words_view(dram):
            return dram[0].rearrange("p n t -> p (n t)").bitcast(I32)

        def load_list(dram, n, name):
            t = keep.tile([P, n // 16], U16, name=name)
            nc.sync.dma_start(t[:], dram)
            return t

        d_sc = sb([P, G], U8, "d_sc")
        x_sc = sb([P, T], U8, "x_sc")
        nc.gpsimd.memset(d_sc[:].bitcast(I32), 0)
        nc.vector.memset(x_sc[:].bitcast(I32), 0)

        k1_sb = load_list(k1, H, "k1_sb")
        nc.sync.dma_start(d_sc[:].bitcast(I32)[0:P:8, :], d_scales[0].bitcast(I32))
        for r in range(4):
            nc.sync.dma_start(x_sc[:].bitcast(I32)[r:P:32, :], x_scales[0].bitcast(I32)[r:16:4, :])
        offs_sb = load_list(offs, S, "offs_sb")
        d_w = sb([P, G], U32, "d_w")
        nc.sync.dma_start(d_w[:].bitcast(I32), words_view(d_words))
        x_w = sb([P, T], U32, "x_w")
        nc.sync.dma_start(x_w[:].bitcast(I32), words_view(x_words))
        two_sb = load_list(two, S, "two_sb")
        n1_sb = load_list(n1, W, "n1_sb")
        n2_sb = load_list(n2, U, "n2_sb")
        n3_sb = load_list(n3, U, "n3_sb")
        gain = sb([P, PACK], F32, "gain")
        nc.gpsimd.dma_start(gain[:], gn.rearrange("(p t) o -> p (t o)", t=PACK))

        s_win = [sb([P, S_WIN], F32, f"s_win{t}") for t in range(PACK)]
        h_win = [sb([P, H_WIN], F32, f"h_win{t}") for t in range(PACK)]
        for t in range(PACK):
            nc.gpsimd.memset(s_win[t][:, S:S_WIN], 0.0)
            nc.gpsimd.memset(h_win[t][:, S:H_WIN], 0.0)

        gain16 = sb([P, PACK], F32, "gain16")
        nc.scalar.activation(gain16[:], gain[:], COPY, scale=0.0625)

        def deal(dst, src):
            nc.vector.tensor_copy(
                dst.rearrange("p (w t m) -> p w m t", t=PACK, m=P),
                src.rearrange("p (w m t) -> p w m t", t=PACK, m=P),
            )

        dk_sc_raw = sb([P, H], U8, "dk_sc_raw")
        nc.vector.tensor_copy(dk_sc_raw[:], d_sc[:].indirect(k1_sb[:]))
        dk_sc_dealt = sb([P, H], U8, "dk_sc_dealt")
        deal(dk_sc_dealt[:], dk_sc_raw[:])
        dk_sc = sb([P, H], U8, "dk_sc")
        nc.vector.tensor_copy(dk_sc[:].bitcast(I32), dk_sc_dealt[:].bitcast(I32))
        for r in range(1, 4):
            nc.scalar.dma_start(dk_sc[:].bitcast(I32)[r:P:32, :], dk_sc_dealt[:].bitcast(I32)[8 * r : P : 32, :])

        xq_sc = sb([P, S], U8, "xq_sc")
        nc.vector.tensor_copy(xq_sc[:], x_sc[:].indirect(offs_sb[:]))
        dk_w_raw = sb([P, H], U32, "dk_w_raw")
        nc.vector.tensor_copy(dk_w_raw[:], d_w[:].indirect(k1_sb[:]))
        w_w = sb([P, 2 * N], U32, "d_w")
        nc.sync.dma_start(w_w[:, 0:N].bitcast(I32), words_view(w1_words))
        nc.sync.dma_start(w_w[:, N : 2 * N].bitcast(I32), words_view(w2_words))
        dk_w = sb([P, H], U32, "dk_w")
        deal(dk_w[:].bitcast(I32), dk_w_raw[:].bitcast(I32))
        w_sc = sb([P, N], U8, "dk_w_raw")
        nc.gpsimd.memset(w_sc[:].bitcast(I32), 0)
        for j, sc in enumerate((w1_scales, w2_scales)):
            for q in range(4):
                nc.sync.dma_start(
                    w_sc[:].bitcast(I32)[32 * q + 4 * j : 32 * q + 4 * j + 4, :],
                    sc[0].bitcast(I32)[4 * q : 4 * q + 4, :],
                )
        xq_w = sb([P, S], U32, "xq_w")
        nc.vector.tensor_copy(xq_w[:], x_w[:].indirect(offs_sb[:]))

        s_ps = []
        for t in range(PACK):
            ps = psum.tile([P, S], F32, name=f"bank{t}")
            cols = slice(P * t, P * (t + 1))
            nc.tensor.matmul_mx(ps[:], lhsT=dk_w[:, cols].bitcast(FP8X4), lhsT_scale=dk_sc[:, cols],
                                rhs=xq_w[:].bitcast(FP8X4), rhs_scale=xq_sc[:], start=True, stop=True)
            s_ps.append(ps)

        x2_w = sb([P, S], U32, "x2_w")
        nc.vector.tensor_copy(x2_w[:], x_w[:].indirect(two_sb[:]))
        wd_w = sb([P, 2 * N], U32, "wd_w")
        wd_sc = sb([P, N], U8, "wd_sc")
        deal(wd_w[:].bitcast(I32), w_w[:].bitcast(I32))
        nc.scalar.activation(s_win[0][:, 0:S], s_ps[0][:], COPY)
        for t in (1, 2):
            nc.vector.tensor_copy(s_win[t][:, 0:S], s_ps[t][:])
        x2_sc = sb([P, S], U8, "x2_sc")
        nc.vector.tensor_copy(x2_sc[:], x_sc[:].indirect(two_sb[:]))

        units = [(c, t) for c in range(NCH) for t in range(PACK)]
        members = [sb([P, 2 * CH], F32, f"members{u}") for u in range(len(units))]
        top = [sb([P, CH], F32, f"top{u}") for u in range(len(units))]
        gap = [sb([P, CH], F32, f"gap{u}") for u in range(len(units))]
        diff = [sb([P, CH], F32, f"diff{u}") for u in range(len(units))]
        z_rows = sb([P, PACK * CH], BF16, "z_rows")
        z_grp = [sb([P, PACK * CH], BF16, f"z_grp{c}") for c in range(NCH)]
        z_w = [sb([P, CH], U32, f"z_w{c}") for c in range(NCH)]
        z_sc = [sb([P, CH], U8, f"z_sc{c}") for c in range(NCH)]
        h_ps = {}

        def interleave(eng_copy, dst, src):
            eng_copy(dst.rearrange("p (c i t) -> p c t i", i=4, t=PACK), src.rearrange("p t (c i) -> p c t i", i=4))

        def interleave_scalar(dst, src):
            nc.scalar.copy(dst.rearrange("p (c t) -> p c t", t=PACK), src.rearrange("p t c -> p c t"))

        def interleave_vector(dst, src):
            interleave(nc.vector.tensor_copy, dst, src)

        def fetch(u):
            c, t = units[u]
            nc.scalar.activation(members[u][:], s_win[t][:].indirect(n1_sb[:, c * CH // 8 : (c + 1) * CH // 8]), COPY)

        def op_top(u):
            c, t = units[u]
            nc.vector.tensor_tensor(top[u][:], members[u][:, 1::2], s_win[t][:, c * CH : (c + 1) * CH], ALU.max)

        def op_gap(u):
            nc.vector.tensor_tensor(gap[u][:], members[u][:, 0::2], top[u][:], ALU.subtract)

        def op_diff(u):
            nc.vector.scalar_tensor_tensor(diff[u][:], gap[u][:], 0.0, members[u][:, 1::2], ALU.min, ALU.add)

        def gain_rows(t):
            nc.vector.tensor_scalar(z_rows[:, t * CH : (t + 1) * CH], diff[t][:], gain16[:, t : t + 1], None, ALU.mult)

        def gain_grouped(t):
            if t < 2:
                nc.scalar.activation(z_grp[1][:, t::PACK], diff[PACK + t][:], COPY, scale=gain16[:, t : t + 1])
            else:
                nc.vector.tensor_scalar(z_grp[1][:, t::PACK], diff[PACK + t][:], gain16[:, t : t + 1], None, ALU.mult)

        def quant_z(c):
            nc.vector.quantize_mx(z_w[c][:].bitcast(FP8X4), z_sc[c][:], z_grp[c][:])

        def open_h(c, t):
            ccols = slice(c * CH, (c + 1) * CH)
            ps = psum.tile([P, CH], F32, name=f"bank{(4 * (1 - c)) + t}")
            h_ps[c, t] = ps
            nc.tensor.matmul_mx(ps[:], lhsT=wd_w[:, N + P * t : N + P * (t + 1)].bitcast(FP8X4),
                                lhsT_scale=wd_sc[4:P, P * t : P * (t + 1)],
                                rhs=x2_w[:, ccols].bitcast(FP8X4), rhs_scale=x2_sc[:, ccols], start=True, stop=False)

        def close_h(c, t):
            nc.tensor.matmul_mx(h_ps[c, t][:], lhsT=wd_w[:, P * t : P * (t + 1)].bitcast(FP8X4),
                                lhsT_scale=wd_sc[:, P * t : P * (t + 1)],
                                rhs=z_w[c][:].bitcast(FP8X4), rhs_scale=z_sc[c][:], start=False, stop=True)

        for u in range(len(units)):
            if u == 2:
                nc.scalar.activation(s_win[3][:, 0:S], s_ps[3][:], COPY)
            fetch(u)
        for u in range(len(units) + 1):
            if u < len(units):
                op_top(u)
            if u > 0:
                op_diff(u - 1)
            if u < len(units):
                op_gap(u)
            if 0 < u <= PACK:
                gain_rows(u - 1)
            if u == 1:
                deal(wd_sc[:], w_sc[:])
                for c in range(NCH):
                    for t in range(PACK):
                        open_h(c, t)
            if u == PACK:
                interleave_scalar(z_grp[0][:], z_rows[:].rearrange("p (t c) -> p t c", t=PACK))
            if u > PACK:
                gain_grouped(u - 1 - PACK)
            if u == len(units) - 1:
                quant_z(0)
                for t in range(PACK):
                    close_h(0, t)
                    nc.scalar.copy(h_win[t][:, 0:CH], h_ps[0, t][:])
        quant_z(1)
        for t in (0, 1, 3, 2):
            close_h(1, t)

        old = [sb([P, U], F32, f"old{t}") for t in range(PACK)]
        pull = [sb([P, U], F32, f"pull{t}") for t in range(PACK)]
        out_rows = out_0.rearrange("(p t) c -> p t c", t=PACK)

        def pull_of(t):
            nc.scalar.activation(pull[t][:], h_win[t][:].indirect(n3_sb[:]), COPY, scale=-0.5)

        def old_of(t):
            nc.scalar.activation(old[t][:], h_win[t][:].indirect(n2_sb[:]), COPY)

        def put(t):
            nc.vector.tensor_tensor(h_win[t][:].indirect(n2_sb[:]), old[t][:], pull[t][:], ALU.add)

        def store(t):
            nc.sync.dma_start(out_rows[:, t, :], h_win[t][:, 0:S])

        def h_out(eng_copy, t):
            eng_copy(h_win[t][:, CH:S], h_ps[1, t][:])

        def round_rows(eng_copy, o_rows, t):
            eng_copy(o_rows[:, t * S : (t + 1) * S], h_win[t][:, 0:S])

        h_out(nc.scalar.copy, 0)
        h_out(nc.vector.tensor_copy, 1)
        pull_of(0)
        nc.vector.tensor_copy(old[0][:], h_win[0][:].indirect(n2_sb[:]))
        put(0)
        store(0)
        h_out(nc.scalar.copy, 3)
        h_out(nc.scalar.copy, 2)
        pull_of(3)
        nc.vector.tensor_tensor(old[3][:], h_win[3][:].indirect(n2_sb[:]), pull[3][:], ALU.add)
        old_of(1)
        pull_of(1)
        put(1)
        store(1)
        old_of(2)
        pull_of(2)
        put(2)
        store(2)
        nc.scalar.activation(h_win[3][:].indirect(n2_sb[:]), old[3][:], COPY)
        store(3)
        o_rows = sb([P, PACK * S], BF16, "old3")
        round_rows(nc.scalar.copy, o_rows, 0)
        round_rows(nc.scalar.copy, o_rows, 3)
        round_rows(nc.vector.tensor_copy, o_rows, 1)
        round_rows(nc.vector.tensor_copy, o_rows, 2)

        o_grp = sb([P, PACK * S], BF16, "o_grp")
        o_w = sb([P, S], U32, "o_w")
        o_sc = sb([P, S], U8, "o_sc")
        o_view = o_rows[:].rearrange("p (t c) -> p t c", t=PACK)
        for regroup, lo, hi in ((interleave_vector, 0, CH), (interleave_scalar, SPLIT, S), (interleave_vector, CH, SPLIT)):
            regroup(o_grp[:, PACK * lo : PACK * hi], o_view[:, :, lo:hi])
        for c in range(2):
            ccols = slice(c * CH, (c + 1) * CH)
            nc.vector.quantize_mx(o_w[:, ccols].bitcast(FP8X4), o_sc[:, ccols], o_grp[:, PACK * c * CH : PACK * (c + 1) * CH])
            nc.sync.dma_start(words_view(out_1)[:, ccols], o_w[:, ccols].bitcast(I32))
        for q in range(4):
            eng = nc.sync if q % 2 == 0 else nc.scalar
            eng.dma_start(out_2[0].bitcast(I32)[4 * q : 4 * q + 4, :], o_sc[:].bitcast(I32)[32 * q : 32 * q + 4, :])
